import numpy as np
import ml_dtypes


def mxq(x, axis, fmt="e4m3"):
    dtype, down = {"e4m3": (ml_dtypes.float8_e4m3fn, 7), "e5m2": (ml_dtypes.float8_e5m2, 14)}[fmt]
    v = np.moveaxis(np.asarray(x, np.float32).astype(ml_dtypes.bfloat16).astype(np.float64), axis, -1)
    blocks = v.reshape(v.shape[:-1] + (-1, 32))
    amax = np.abs(blocks).max(-1, keepdims=True)
    byte = np.maximum(np.where(amax > 0, np.frexp(amax)[1] - 1 + 127, 0) - down, 1)
    scale = np.exp2(byte - 127.0)
    codes = (blocks / scale).astype(np.float32).astype(dtype).astype(np.float64)
    return np.moveaxis((codes * scale).reshape(v.shape), -1, axis)


WIDE = False


def mx_kscale(k):
    if not WIDE:
        return np.ones(k)
    levels = np.array([10, -10, 5, -5, 0])
    if k % 512:
        return np.exp2(np.random.permutation(np.resize(levels, k // 32))).repeat(32)
    a = np.empty((k // 512, 16))
    for p in range(k // 512):
        a[p, :8] = np.random.permutation(np.resize(levels, 8))
        for g in range(8):
            far = levels[np.abs(levels - a[p, g]) >= 10]
            a[p, g + 8] = far[np.random.randint(len(far))]
    return np.exp2(a.ravel()).repeat(32)


def f64(x):
    return np.asarray(x).astype(np.float64)


def striped(idx):
    return np.tile(idx.reshape(-1, 16).T, (8, 1)).astype(np.uint16)


def unstriped(offs):
    return offs[:16].T.reshape(-1).astype(np.int64)


def striped8(idx):
    return np.concatenate([x.reshape(-1, 16).T for x in idx]).astype(np.uint16)


def runs(offs, k):
    lists = np.stack([offs[16 * r : 16 * r + 16].T.reshape(-1) for r in range(8)]).astype(np.int64)
    return lists[np.arange(k) % 512 // 64]


def pack_weight(w):
    k, n = w.shape
    w = f64(np.asarray(w, np.float32).astype(ml_dtypes.bfloat16)).reshape(k // 32, 32, n)
    amax = np.abs(w).max(1)
    byte = np.clip(np.where(amax > 0, np.frexp(amax)[1] - 1 + 127 - 7, 1), 1, 254)
    scaled = (w * np.exp2(127.0 - byte)[:, None, :]).reshape(k, n).astype(np.float32)
    words = np.ascontiguousarray(scaled.reshape(k // 512, 128, 4, n).transpose(0, 1, 3, 2)).astype(ml_dtypes.float8_e4m3fn).view(np.uint8)
    return words, np.ascontiguousarray(byte.astype(np.uint8).reshape(k // 512, 16, n))


def unpack_weight(words, scales):
    g, p, n, _ = words.shape
    vals = np.ascontiguousarray(words).view(ml_dtypes.float8_e4m3fn).astype(np.float64) * np.repeat(np.exp2(scales.astype(np.float64) - 127.0), 8, axis=1)[..., None]
    return vals.transpose(0, 1, 3, 2).reshape(g * 512, n)


def sigmoid(v):
    return 1.0 / (1.0 + np.exp(-np.maximum(v, -700.0)))


K, T, S, N, H = 512, 2048, 512, 512, 512


def setup_inputs():
    n = np.random.standard_normal
    s = mx_kscale(K)[:, None]
    u = mx_kscale(H)
    packed_xT = pack_weight(n((K, T)) * s)
    return {
        "x_words": packed_xT[0],
        "x_scales": packed_xT[1],
        "w1": (n((K, H)) / np.sqrt(K) / s).astype(np.float32),
        "gn": (np.random.uniform(0.5, 1.5, (H, 1)) * u[:, None]).astype(np.float32),
        "w2": (n((H, N)) / np.sqrt(H) / u[:, None]).astype(np.float32),
        "offs": striped(np.random.permutation(T)[:S]),
        "n1": striped8(np.stack([np.random.permutation(S) for _ in range(8)])),
        "n2": striped8(np.stack([np.random.permutation(S) for _ in range(8)])),
        "n3": striped8(np.stack([np.random.permutation(S) for _ in range(8)])),
        "n4": striped8(np.stack([np.random.permutation(S) for _ in range(8)])),
    }


def reference(x_words, x_scales, w1, gn, w2, offs, n1, n2, n3, n4):
    xq = unpack_weight(x_words, x_scales)[:, unstriped(offs)]
    y = mxq(f64(w1), 0, "e4m3").T @ xq
    pa = y[np.arange(H)[:, None], runs(n1, H)]
    pb = y[np.arange(H)[:, None], runs(n2, H)]
    z = f64(gn) * (np.maximum(np.minimum(y, pa), np.minimum(np.maximum(y, pa), pb)))
    h = mxq(f64(w2), 0, "e4m3").T @ mxq(z, 0, "e4m3")
    sm = np.maximum(h, h[np.arange(N)[:, None], runs(n4, N)])
    ds = np.zeros((N, S))
    ds[np.arange(N)[:, None], runs(n3, N)] = sm
    return ds * sigmoid(h)

@@ -1,0 +1,217 @@
+from contextlib import ExitStack
+
+import concourse.mybir as mybir
+
+K, T, S, H, N = 512, 2048, 512, 512, 512
+FLOPS = 2 * K * H * S + 2 * H * N * S
+
+F32 = mybir.dt.float32
+BF16 = mybir.dt.bfloat16
+I32 = mybir.dt.int32
+U32 = mybir.dt.uint32
+U16 = mybir.dt.uint16
+U8 = mybir.dt.uint8
+FP8X4 = mybir.dt.float8_e4m3fn_x4
+ALU = mybir.AluOpType
+ACT = mybir.ActivationFunctionType
+
+P = 128
+PACK = 4
+HALF = S // 2
+LC = HALF // 16
+
+
+def tile_picked_laymedsendg_none_p_kernel(
+    tc, x_words, x_scales, w1, gn, w2, offs, n1, n2, n3, n4, out
+):
+    nc = tc.nc
+    with ExitStack() as ctx:
+        lists = ctx.enter_context(tc.tile_pool(name="lists", bufs=1))
+        keep = ctx.enter_context(tc.tile_pool(name="keep", bufs=1))
+        psum = ctx.enter_context(tc.psum_pool(name="psum", bufs=1))
+
+        def load_list(src, name):
+            tile = lists.tile([P, S // 16], U16, name=name)
+            nc.sync.dma_start(tile[:], src)
+            return tile
+
+        def load_weight_half(w, half, name):
+            raw = keep.tile([P, PACK, HALF], F32, name=name)
+            nc.sync.dma_start(raw[:], w.rearrange("(p j) c -> p j c", j=PACK)[:, :, half * HALF : (half + 1) * HALF])
+            return raw
+
+        def deal_views(dealt, raw, half):
+            m = slice(half * (P // 2), (half + 1) * (P // 2))
+            return dealt[:, :, m, :].rearrange("p t m j -> p m j t"), raw[:].rearrange("p j (m t) -> p m j t", t=PACK)
+
+        def quantize_weight_tile(dealt, codes, scales, t):
+            nc.vector.quantize_mx(
+                out=codes[:, t * P : (t + 1) * P].bitcast(FP8X4),
+                scales=scales[:, t * P : (t + 1) * P],
+                in_=dealt[:, t, :, :].rearrange("p m j -> p (m j)"),
+            )
+
+        x_bytes = keep.tile([P, T], U8, name="x_bytes")
+        nc.vector.memset(x_bytes[:].bitcast(I32), 0)
+        offs_sb = load_list(offs, "offs_sb")
+        x_table = keep.tile([P, T], U32, name="x_table")
+        nc.sync.dma_start(x_table[:].bitcast(I32), x_words[0].rearrange("p n r -> p (n r)").bitcast(I32))
+        for q in range(4):
+            nc.sync.dma_start(
+                x_bytes[32 * q : 32 * q + 4, :].bitcast(I32), x_scales[0, 4 * q : 4 * q + 4, :].bitcast(I32)
+            )
+        w1_raw = [load_weight_half(w1, half, "w1_raw%d" % half) for half in range(2)]
+        gain = keep.tile([P, PACK], F32, name="gain")
+        nc.sync.dma_start(gain[:], gn.rearrange("(p t) o -> p (t o)", t=PACK))
+        n1_sb = load_list(n1, "n1_sb")
+        n2_sb = load_list(n2, "n2_sb")
+        w2_raw = [load_weight_half(w2, half, "w2_raw%d" % half) for half in range(2)]
+        n4_sb = load_list(n4, "n4_sb")
+        n3_sb = load_list(n3, "n3_sb")
+
+        xq_codes = keep.tile([P, S], U32, name="xq_codes", align_bytes=64)
+        xq_scales = keep.tile([P, S], U8, name="xq_scales", align_bytes=64)
+        nc.vector.tensor_copy(xq_codes[:], x_table[:].indirect(offs_sb[:]))
+        nc.vector.tensor_copy(xq_scales[:], x_bytes[:].indirect(offs_sb[:]))
+
+        w1_dealt = keep.tile([P, PACK, P, PACK], BF16, name="w1_dealt", align_bytes=64)
+        nc.scalar.copy(*deal_views(w1_dealt, w1_raw[0], 0))
+        nc.vector.tensor_copy(*deal_views(w1_dealt, w1_raw[1], 1))
+        w1_codes = keep.tile([P, H], U32, name="w1_codes", align_bytes=64)
+        w1_scales = keep.tile([P, H], U8, name="w1_scales", align_bytes=64)
+        y_ps = []
+        for t in range(PACK):
+            quantize_weight_tile(w1_dealt, w1_codes, w1_scales, t)
+            acc = psum.tile([P, S], F32, name="y_ps%d" % t, tag="bank%d" % t)
+            nc.tensor.matmul_mx(
+                out=acc[:],
+                lhsT=w1_codes[:, t * P : (t + 1) * P].bitcast(FP8X4),
+                lhsT_scale=w1_scales[:, t * P : (t + 1) * P],
+                rhs=xq_codes[:].bitcast(FP8X4),
+                rhs_scale=xq_scales[:],
+                start=True,
+                stop=True,
+            )
+            y_ps.append(acc)
+
+        gy = [keep.tile([P, S], F32, name="gy%d" % t) for t in range(PACK)]
+        for t in range(PACK):
+            nc.scalar.activation(gy[t][:], y_ps[t][:], ACT.Copy, scale=gain[:, t : t + 1])
+        gy_bf = keep.tile([P, 2, PACK, HALF], BF16, name="gy_bf")
+        for t in range(PACK):
+            nc.scalar.activation(
+                gy_bf[:, :, t, :], y_ps[t][:].rearrange("p (c j) -> p c j", c=2), ACT.Copy, scale=gain[:, t : t + 1]
+            )
+
+        w2_dealt = keep.tile([P, PACK, P, PACK], BF16, name="w2_dealt", align_bytes=64)
+        for half in range(2):
+            nc.scalar.copy(*deal_views(w2_dealt, w2_raw[half], half))
+        w2_codes = keep.tile([P, N], U32, name="w2_codes", align_bytes=64)
+        w2_scales = keep.tile([P, N], U8, name="w2_scales", align_bytes=64)
+
+        h_win = [keep.tile([P, S], F32, name="h_win%d" % t) for t in range(PACK)]
+        h_own = [keep.tile([P, S], F32, name="h_own%d" % t) for t in range(PACK)]
+        gate = [keep.tile([P, S], F32, name="gate%d" % t) for t in range(PACK)]
+
+        def weave(ap):
+            return ap.rearrange("p t (c i) -> p c t i", i=4)
+
+        def woven(ap):
+            return ap.rearrange("p (c i) t -> p c t i", i=4)
+
+        def fetch_y(c, t, dst, places):
+            nc.vector.tensor_copy(dst[:, t, :], gy[t][:].indirect(places[:, c * LC : (c + 1) * LC]))
+
+        def bounds(c, pa, pb):
+            lo = keep.tile([P, PACK, HALF], BF16, name="lo%d" % c)
+            hi = keep.tile([P, PACK, HALF], BF16, name="hi%d" % c)
+            cut = keep.tile([P, PACK, HALF], BF16, name="cut%d" % c)
+            nc.vector.tensor_tensor(hi[:], pa[:], pb[:], ALU.max)
+            nc.vector.tensor_tensor(lo[:], pa[:], pb[:], ALU.min)
+            nc.vector.tensor_tensor(cut[:], hi[:], gy_bf[:, c, :, :], ALU.min)
+            return lo, cut
+
+        def second_product(c, z):
+            z_codes = keep.tile([P, HALF], U32, name="z_codes%d" % c, align_bytes=64)
+            z_scales = keep.tile([P, HALF], U8, name="z_scales%d" % c, align_bytes=64)
+            nc.vector.quantize_mx(
+                out=z_codes[:].bitcast(FP8X4), scales=z_scales[:], in_=z[:].rearrange("p j t -> p (j t)")
+            )
+            banks = []
+            for t in range(PACK):
+                acc = psum.tile([P, HALF], F32, name="h_ps%d_%d" % (c, t), tag="bank%d" % (t + PACK * (1 - c)))
+                nc.tensor.matmul_mx(
+                    out=acc[:],
+                    lhsT=w2_codes[:, t * P : (t + 1) * P].bitcast(FP8X4),
+                    lhsT_scale=w2_scales[:, t * P : (t + 1) * P],
+                    rhs=z_codes[:].bitcast(FP8X4),
+                    rhs_scale=z_scales[:],
+                    start=True,
+                    stop=True,
+                )
+                banks.append(acc)
+            return banks
+
+        def leave_bank(c, t, acc):
+            cols = slice(c * HALF, (c + 1) * HALF)
+            nc.scalar.copy(h_win[t][:, cols], acc[:])
+            nc.scalar.copy(h_own[t][:, cols], acc[:])
+
+        pa = keep.tile([P, PACK, HALF], BF16, name="pa0")
+        pb = keep.tile([P, PACK, HALF], BF16, name="pb0")
+        for t in range(PACK):
+            fetch_y(0, t, pa, n1_sb)
+            fetch_y(0, t, pb, n2_sb)
+        lo, cut = bounds(0, pa, pb)
+        z_planes = keep.tile([P, PACK, HALF], BF16, name="z_planes")
+        nc.vector.tensor_tensor(z_planes[:], lo[:], cut[:], ALU.max)
+        z0 = keep.tile([P, HALF, PACK], BF16, name="z0", tag="z0_then_pb1", align_bytes=64)
+        nc.scalar.copy(woven(z0[:]), weave(z_planes[:]))
+        for t in range(PACK):
+            quantize_weight_tile(w2_dealt, w2_codes, w2_scales, t)
+        pa = keep.tile([P, PACK, HALF], BF16, name="pa1")
+        for t in range(PACK):
+            fetch_y(1, t, pa, n1_sb)
+        banks = second_product(0, z0)
+        pb = keep.tile([P, PACK, HALF], BF16, name="pb1", tag="z0_then_pb1", align_bytes=64)
+        for t in range(PACK):
+            fetch_y(1, t, pb, n2_sb)
+        for t in range(PACK):
+            leave_bank(0, t, banks[t])
+        lo, cut = bounds(1, pa, pb)
+        z1 = keep.tile([P, HALF, PACK], BF16, name="z1", align_bytes=64)
+        nc.vector.tensor_tensor(woven(z1[:]), weave(lo[:]), weave(cut[:]), ALU.max)
+        banks = second_product(1, z1)
+
+        out_rows = out.rearrange("(p t) c -> p t c", t=PACK)
+        rise = [keep.tile([P, S], F32, name="rise%d" % t) for t in range(PACK)]
+        lift = [keep.tile([P, S], F32, name="lift%d" % t) for t in range(PACK)]
+        sent = [keep.tile([P, 2 * S], F32, name="sent%d" % t) for t in range(PACK)]
+        res = [keep.tile([P, S], F32, name="res%d" % t) for t in range(PACK)]
+
+        def fetch(t):
+            leave_bank(1, t, banks[t])
+            for c in range(2):
+                cols = slice(c * HALF, (c + 1) * HALF)
+                nc.vector.tensor_tensor(
+                    rise[t][:, cols], h_win[t][:].indirect(n4_sb[:, c * LC : (c + 1) * LC]), h_own[t][:, cols], ALU.subtract
+                )
+
+        def send(t):
+            nc.scalar.activation(lift[t][:], rise[t][:], ACT.Relu)
+            nc.scalar.activation(gate[t][:], h_own[t][:], ACT.Sigmoid)
+            nc.vector.tensor_tensor(sent[t][:].indirect(n3_sb[:]), h_own[t][:], lift[t][:], ALU.add)
+
+        def finish(t):
+            nc.vector.tensor_tensor(res[t][:], sent[t][:, 0:S], gate[t][:], ALU.mult)
+            nc.sync.dma_start(out_rows[:, t, :], res[t][:])
+
+        fetch(0)
+        fetch(1)
+        for t in range(PACK):
+            send(t)
+            if t + 2 < PACK:
+                fetch(t + 2)
+            if t >= 1:
+                finish(t - 1)
+        finish(PACK - 1)

@@ -18,7 +18,9 @@ ACT = mybir.ActivationFunctionType
 P = 128
 PACK = 4
 HALF = S // 2
+QUARTER = S // 4
 LC = HALF // 16
+VECTOR_SHARE = 44
 
 
 def tile_picked_laymedsendg_none_p_kernel(
@@ -40,9 +42,12 @@ def tile_picked_laymedsendg_none_p_kernel(
             nc.sync.dma_start(raw[:], w.rearrange("(p j) c -> p j c", j=PACK)[:, :, half * HALF : (half + 1) * HALF])
             return raw
 
-        def deal_views(dealt, raw, half):
-            m = slice(half * (P // 2), (half + 1) * (P // 2))
-            return dealt[:, :, m, :].rearrange("p t m j -> p m j t"), raw[:].rearrange("p j (m t) -> p m j t", t=PACK)
+        def deal_views(dealt, raw, half, m0, m1):
+            first = half * (P // 2)
+            return (
+                dealt[:, :, first + m0 : first + m1, :].rearrange("p t m j -> p m j t"),
+                raw[:, :, PACK * m0 : PACK * m1].rearrange("p j (m t) -> p m j t", t=PACK),
+            )
 
         def quantize_weight_tile(dealt, codes, scales, t):
             nc.vector.quantize_mx(
@@ -75,37 +80,41 @@ def tile_picked_laymedsendg_none_p_kernel(
         nc.vector.tensor_copy(xq_scales[:], x_bytes[:].indirect(offs_sb[:]))
 
         w1_dealt = keep.tile([P, PACK, P, PACK], BF16, name="w1_dealt", align_bytes=64)
-        nc.scalar.copy(*deal_views(w1_dealt, w1_raw[0], 0))
-        nc.vector.tensor_copy(*deal_views(w1_dealt, w1_raw[1], 1))
+        nc.scalar.copy(*deal_views(w1_dealt, w1_raw[0], 0, 0, P // 2))
+        nc.vector.tensor_copy(*deal_views(w1_dealt, w1_raw[1], 1, 0, VECTOR_SHARE))
+        nc.scalar.copy(*deal_views(w1_dealt, w1_raw[1], 1, VECTOR_SHARE, P // 2))
         w1_codes = keep.tile([P, H], U32, name="w1_codes", align_bytes=64)
         w1_scales = keep.tile([P, H], U8, name="w1_scales", align_bytes=64)
-        y_ps = []
+        gy = [keep.tile([P, S], F32, name="gy%d" % t) for t in range(PACK)]
+        gy_bf = [keep.tile([P, PACK, HALF], BF16, name="gy_bf%d" % c) for c in range(2)]
+        y_ps = {}
         for t in range(PACK):
             quantize_weight_tile(w1_dealt, w1_codes, w1_scales, t)
-            acc = psum.tile([P, S], F32, name="y_ps%d" % t, tag="bank%d" % t)
-            nc.tensor.matmul_mx(
-                out=acc[:],
-                lhsT=w1_codes[:, t * P : (t + 1) * P].bitcast(FP8X4),
-                lhsT_scale=w1_scales[:, t * P : (t + 1) * P],
-                rhs=xq_codes[:].bitcast(FP8X4),
-                rhs_scale=xq_scales[:],
-                start=True,
-                stop=True,
-            )
-            y_ps.append(acc)
-
-        gy = [keep.tile([P, S], F32, name="gy%d" % t) for t in range(PACK)]
+            for c in range(2):
+                cols = slice(c * HALF, (c + 1) * HALF)
+                acc = psum.tile([P, HALF], F32, name="y_ps%d_%d" % (c, t), tag="bank%d" % (t + PACK * c))
+                nc.tensor.matmul_mx(
+                    out=acc[:],
+                    lhsT=w1_codes[:, t * P : (t + 1) * P].bitcast(FP8X4),
+                    lhsT_scale=w1_scales[:, t * P : (t + 1) * P],
+                    rhs=xq_codes[:, cols].bitcast(FP8X4),
+                    rhs_scale=xq_scales[:, cols],
+                    start=True,
+                    stop=True,
+                )
+                y_ps[PACK * c + t] = acc
         for t in range(PACK):
-            nc.scalar.activation(gy[t][:], y_ps[t][:], ACT.Copy, scale=gain[:, t : t + 1])
-        gy_bf = keep.tile([P, 2, PACK, HALF], BF16, name="gy_bf")
-        for t in range(PACK):
-            nc.scalar.activation(
-                gy_bf[:, :, t, :], y_ps[t][:].rearrange("p (c j) -> p c j", c=2), ACT.Copy, scale=gain[:, t : t + 1]
-            )
+            for c in range(2):
+                nc.scalar.activation(
+                    gy[t][:, c * HALF : (c + 1) * HALF], y_ps[PACK * c + t][:], ACT.Copy, scale=gain[:, t : t + 1]
+                )
+        for c in range(2):
+            for t in range(PACK):
+                nc.scalar.activation(gy_bf[c][:, t, :], y_ps[PACK * c + t][:], ACT.Copy, scale=gain[:, t : t + 1])
 
         w2_dealt = keep.tile([P, PACK, P, PACK], BF16, name="w2_dealt", align_bytes=64)
         for half in range(2):
-            nc.scalar.copy(*deal_views(w2_dealt, w2_raw[half], half))
+            nc.scalar.copy(*deal_views(w2_dealt, w2_raw[half], half, 0, P // 2))
         w2_codes = keep.tile([P, N], U32, name="w2_codes", align_bytes=64)
         w2_scales = keep.tile([P, N], U8, name="w2_scales", align_bytes=64)
 
@@ -125,21 +134,21 @@ def tile_picked_laymedsendg_none_p_kernel(
         def bounds(c, pa, pb):
             lo = keep.tile([P, PACK, HALF], BF16, name="lo%d" % c)
             hi = keep.tile([P, PACK, HALF], BF16, name="hi%d" % c)
-            cut = keep.tile([P, PACK, HALF], BF16, name="cut%d" % c)
+            cut = keep.tile([P, PACK, HALF], BF16, name="cut%d" % c, tag="cut0_then_pa1" if c == 0 else "cut1")
             nc.vector.tensor_tensor(hi[:], pa[:], pb[:], ALU.max)
             nc.vector.tensor_tensor(lo[:], pa[:], pb[:], ALU.min)
-            nc.vector.tensor_tensor(cut[:], hi[:], gy_bf[:, c, :, :], ALU.min)
+            nc.vector.tensor_tensor(cut[:], hi[:], gy_bf[c][:], ALU.min)
             return lo, cut
 
-        def second_product(c, z):
-            z_codes = keep.tile([P, HALF], U32, name="z_codes%d" % c, align_bytes=64)
-            z_scales = keep.tile([P, HALF], U8, name="z_scales%d" % c, align_bytes=64)
+        def second_product(name, z, width, first_bank):
+            z_codes = keep.tile([P, width], U32, name="z_codes" + name, align_bytes=64)
+            z_scales = keep.tile([P, width], U8, name="z_scales" + name, align_bytes=64)
             nc.vector.quantize_mx(
                 out=z_codes[:].bitcast(FP8X4), scales=z_scales[:], in_=z[:].rearrange("p j t -> p (j t)")
             )
             banks = []
             for t in range(PACK):
-                acc = psum.tile([P, HALF], F32, name="h_ps%d_%d" % (c, t), tag="bank%d" % (t + PACK * (1 - c)))
+                acc = psum.tile([P, width], F32, name="h_ps%s_%d" % (name, t), tag="bank%d" % (t + first_bank))
                 nc.tensor.matmul_mx(
                     out=acc[:],
                     lhsT=w2_codes[:, t * P : (t + 1) * P].bitcast(FP8X4),
@@ -152,8 +161,7 @@ def tile_picked_laymedsendg_none_p_kernel(
                 banks.append(acc)
             return banks
 
-        def leave_bank(c, t, acc):
-            cols = slice(c * HALF, (c + 1) * HALF)
+        def leave_bank(cols, t, acc):
             nc.scalar.copy(h_win[t][:, cols], acc[:])
             nc.scalar.copy(h_own[t][:, cols], acc[:])
 
@@ -167,21 +175,26 @@ def tile_picked_laymedsendg_none_p_kernel(
         nc.vector.tensor_tensor(z_planes[:], lo[:], cut[:], ALU.max)
         z0 = keep.tile([P, HALF, PACK], BF16, name="z0", tag="z0_then_pb1", align_bytes=64)
         nc.scalar.copy(woven(z0[:]), weave(z_planes[:]))
-        for t in range(PACK):
-            quantize_weight_tile(w2_dealt, w2_codes, w2_scales, t)
-        pa = keep.tile([P, PACK, HALF], BF16, name="pa1")
+        nc.vector.quantize_mx(
+            out=w2_codes[:].bitcast(FP8X4), scales=w2_scales[:], in_=w2_dealt[:].rearrange("p t m j -> p (t m j)")
+        )
+        pa = keep.tile([P, PACK, HALF], BF16, name="pa1", tag="cut0_then_pa1")
         for t in range(PACK):
             fetch_y(1, t, pa, n1_sb)
-        banks = second_product(0, z0)
+        banks = second_product("0", z0, HALF, 0)
         pb = keep.tile([P, PACK, HALF], BF16, name="pb1", tag="z0_then_pb1", align_bytes=64)
         for t in range(PACK):
             fetch_y(1, t, pb, n2_sb)
         for t in range(PACK):
-            leave_bank(0, t, banks[t])
+            leave_bank(slice(0, HALF), t, banks[t])
         lo, cut = bounds(1, pa, pb)
-        z1 = keep.tile([P, HALF, PACK], BF16, name="z1", align_bytes=64)
-        nc.vector.tensor_tensor(woven(z1[:]), weave(lo[:]), weave(cut[:]), ALU.max)
-        banks = second_product(1, z1)
+        zq = []
+        for u in range(2):
+            cols = slice(u * QUARTER, (u + 1) * QUARTER)
+            z = keep.tile([P, QUARTER, PACK], BF16, name="z1_%d" % u, align_bytes=64)
+            nc.vector.tensor_tensor(woven(z[:]), weave(lo[:, :, cols]), weave(cut[:, :, cols]), ALU.max)
+            zq.append(z)
+        late_banks = [second_product("1_%d" % u, zq[u], QUARTER, PACK * (1 - u)) for u in range(2)]
 
         out_rows = out.rearrange("(p t) c -> p t c", t=PACK)
         rise = [keep.tile([P, S], F32, name="rise%d" % t) for t in range(PACK)]
@@ -190,7 +203,8 @@ def tile_picked_laymedsendg_none_p_kernel(
         res = [keep.tile([P, S], F32, name="res%d" % t) for t in range(PACK)]
 
         def fetch(t):
-            leave_bank(1, t, banks[t])
+            for u in range(2):
+                leave_bank(slice(HALF + u * QUARTER, HALF + (u + 1) * QUARTER), t, late_banks[u][t])
             for c in range(2):
                 cols = slice(c * HALF, (c + 1) * HALF)
                 nc.vector.tensor_tensor(

@@ -119,7 +119,6 @@ def tile_picked_laymedsendg_none_p_kernel(
         w2_scales = keep.tile([P, N], U8, name="w2_scales", align_bytes=64)
 
         h_win = [keep.tile([P, S], F32, name="h_win%d" % t) for t in range(PACK)]
-        h_own = [keep.tile([P, S], F32, name="h_own%d" % t) for t in range(PACK)]
         gate = [keep.tile([P, S], F32, name="gate%d" % t) for t in range(PACK)]
 
         def weave(ap):
@@ -163,7 +162,6 @@ def tile_picked_laymedsendg_none_p_kernel(
 
         def leave_bank(cols, t, acc):
             nc.scalar.copy(h_win[t][:, cols], acc[:])
-            nc.scalar.copy(h_own[t][:, cols], acc[:])
 
         pa = keep.tile([P, PACK, HALF], BF16, name="pa0")
         pb = keep.tile([P, PACK, HALF], BF16, name="pb0")
@@ -187,6 +185,8 @@ def tile_picked_laymedsendg_none_p_kernel(
             fetch_y(1, t, pb, n2_sb)
         for t in range(PACK):
             leave_bank(slice(0, HALF), t, banks[t])
+        for t in range(PACK):
+            nc.scalar.activation(gate[t][:, 0:HALF], banks[t][:], ACT.Sigmoid)
         lo, cut = bounds(1, pa, pb)
         zq = []
         for u in range(2):
@@ -197,35 +197,31 @@ def tile_picked_laymedsendg_none_p_kernel(
         late_banks = [second_product("1_%d" % u, zq[u], QUARTER, PACK * (1 - u)) for u in range(2)]
 
         out_rows = out.rearrange("(p t) c -> p t c", t=PACK)
-        rise = [keep.tile([P, S], F32, name="rise%d" % t) for t in range(PACK)]
-        lift = [keep.tile([P, S], F32, name="lift%d" % t) for t in range(PACK)]
+        other = [keep.tile([P, S], F32, name="other%d" % t) for t in range(PACK)]
+        larger = [keep.tile([P, S], F32, name="larger%d" % t) for t in range(PACK)]
         sent = [keep.tile([P, 2 * S], F32, name="sent%d" % t) for t in range(PACK)]
-        res = [keep.tile([P, S], F32, name="res%d" % t) for t in range(PACK)]
 
-        def fetch(t):
+        for t in range(PACK):
             for u in range(2):
                 leave_bank(slice(HALF + u * QUARTER, HALF + (u + 1) * QUARTER), t, late_banks[u][t])
             for c in range(2):
                 cols = slice(c * HALF, (c + 1) * HALF)
-                nc.vector.tensor_tensor(
-                    rise[t][:, cols], h_win[t][:].indirect(n4_sb[:, c * LC : (c + 1) * LC]), h_own[t][:, cols], ALU.subtract
-                )
-
-        def send(t):
-            nc.scalar.activation(lift[t][:], rise[t][:], ACT.Relu)
-            nc.scalar.activation(gate[t][:], h_own[t][:], ACT.Sigmoid)
-            nc.vector.tensor_tensor(sent[t][:].indirect(n3_sb[:]), h_own[t][:], lift[t][:], ALU.add)
-
-        def finish(t):
-            nc.vector.tensor_tensor(res[t][:], sent[t][:, 0:S], gate[t][:], ALU.mult)
-            nc.sync.dma_start(out_rows[:, t, :], res[t][:])
-
-        fetch(0)
-        fetch(1)
+                nc.vector.tensor_copy(other[t][:, cols], h_win[t][:].indirect(n4_sb[:, c * LC : (c + 1) * LC]))
         for t in range(PACK):
-            send(t)
-            if t + 2 < PACK:
-                fetch(t + 2)
-            if t >= 1:
-                finish(t - 1)
-        finish(PACK - 1)
+            rise = keep.tile([P, S], F32, name="rise%d" % t, tag="rise")
+            nc.gpsimd.tensor_tensor(rise[:], other[t][:], h_win[t][:], ALU.subtract)
+            lift = keep.tile([P, S], F32, name="lift%d" % t, tag="lift%d" % t)
+            nc.scalar.activation(lift[:], rise[:], ACT.Relu)
+            nc.gpsimd.tensor_tensor(larger[t][:], lift[:], h_win[t][:], ALU.add)
+            nc.vector.tensor_copy(sent[t][:].indirect(n3_sb[:]), larger[t][:])
+            nc.scalar.activation(gate[t][:, HALF:S], h_win[t][:, HALF:S], ACT.Sigmoid)
+        for t in range(PACK - 1):
+            res = keep.tile([P, S], F32, name="res%d" % t, tag="lift%d" % (t + 1))
+            nc.gpsimd.tensor_tensor(res[:], sent[t][:, 0:S], gate[t][:], ALU.mult)
+            nc.sync.dma_start(out_rows[:, t, :], res[:])
+        last = PACK - 1
+        for c in range(2):
+            cols = slice(c * HALF, (c + 1) * HALF)
+            res = keep.tile([P, HALF], F32, name="res_last%d" % c)
+            nc.vector.tensor_tensor(res[:], sent[last][:, cols], gate[last][:, cols], ALU.mult)
+            nc.sync.dma_start(out_rows[:, last, cols], res[:])

@@ -17,10 +17,13 @@ ACT = mybir.ActivationFunctionType
 
 P = 128
 PACK = 4
+QUADRANT = 32
 HALF = S // 2
 QUARTER = S // 4
-LC = HALF // 16
+LIST_HALF = HALF // 16
+RUN = 4
 VECTOR_SHARE = 44
+FUSED = 2
 
 
 def tile_picked_laymedsendg_none_p_kernel(
@@ -49,11 +52,15 @@ def tile_picked_laymedsendg_none_p_kernel(
                 raw[:, :, PACK * m0 : PACK * m1].rearrange("p j (m t) -> p m j t", t=PACK),
             )
 
-        def quantize_weight_tile(dealt, codes, scales, t):
-            nc.vector.quantize_mx(
-                out=codes[:, t * P : (t + 1) * P].bitcast(FP8X4),
-                scales=scales[:, t * P : (t + 1) * P],
-                in_=dealt[:, t, :, :].rearrange("p m j -> p (m j)"),
+        def product(acc, w_codes, w_scales, t, codes, scales):
+            nc.tensor.matmul_mx(
+                out=acc[:],
+                lhsT=w_codes[:, t * P : (t + 1) * P].bitcast(FP8X4),
+                lhsT_scale=w_scales[:, t * P : (t + 1) * P],
+                rhs=codes.bitcast(FP8X4),
+                rhs_scale=scales,
+                start=True,
+                stop=True,
             )
 
         x_bytes = keep.tile([P, T], U8, name="x_bytes")
@@ -61,9 +68,10 @@ def tile_picked_laymedsendg_none_p_kernel(
         offs_sb = load_list(offs, "offs_sb")
         x_table = keep.tile([P, T], U32, name="x_table")
         nc.sync.dma_start(x_table[:].bitcast(I32), x_words[0].rearrange("p n r -> p (n r)").bitcast(I32))
-        for q in range(4):
+        for q in range(P // QUADRANT):
             nc.sync.dma_start(
-                x_bytes[32 * q : 32 * q + 4, :].bitcast(I32), x_scales[0, 4 * q : 4 * q + 4, :].bitcast(I32)
+                x_bytes[QUADRANT * q : QUADRANT * q + 4, :].bitcast(I32),
+                x_scales[0, 4 * q : 4 * q + 4, :].bitcast(I32),
             )
         w1_raw = [load_weight_half(w1, half, "w1_raw%d" % half) for half in range(2)]
         gain = keep.tile([P, PACK], F32, name="gain")
@@ -85,32 +93,28 @@ def tile_picked_laymedsendg_none_p_kernel(
         nc.scalar.copy(*deal_views(w1_dealt, w1_raw[1], 1, VECTOR_SHARE, P // 2))
         w1_codes = keep.tile([P, H], U32, name="w1_codes", align_bytes=64)
         w1_scales = keep.tile([P, H], U8, name="w1_scales", align_bytes=64)
-        gy = [keep.tile([P, S], F32, name="gy%d" % t) for t in range(PACK)]
+        gy = [keep.tile([P, S], F32, name="gy%d" % t, tag="gy%d" % t) for t in range(PACK)]
         gy_bf = [keep.tile([P, PACK, HALF], BF16, name="gy_bf%d" % c) for c in range(2)]
         y_ps = {}
         for t in range(PACK):
-            quantize_weight_tile(w1_dealt, w1_codes, w1_scales, t)
+            nc.vector.quantize_mx(
+                out=w1_codes[:, t * P : (t + 1) * P].bitcast(FP8X4),
+                scales=w1_scales[:, t * P : (t + 1) * P],
+                in_=w1_dealt[:, t, :, :].rearrange("p m j -> p (m j)"),
+            )
             for c in range(2):
                 cols = slice(c * HALF, (c + 1) * HALF)
                 acc = psum.tile([P, HALF], F32, name="y_ps%d_%d" % (c, t), tag="bank%d" % (t + PACK * c))
-                nc.tensor.matmul_mx(
-                    out=acc[:],
-                    lhsT=w1_codes[:, t * P : (t + 1) * P].bitcast(FP8X4),
-                    lhsT_scale=w1_scales[:, t * P : (t + 1) * P],
-                    rhs=xq_codes[:, cols].bitcast(FP8X4),
-                    rhs_scale=xq_scales[:, cols],
-                    start=True,
-                    stop=True,
-                )
-                y_ps[PACK * c + t] = acc
+                product(acc, w1_codes, w1_scales, t, xq_codes[:, cols], xq_scales[:, cols])
+                y_ps[(c, t)] = acc
         for t in range(PACK):
             for c in range(2):
                 nc.scalar.activation(
-                    gy[t][:, c * HALF : (c + 1) * HALF], y_ps[PACK * c + t][:], ACT.Copy, scale=gain[:, t : t + 1]
+                    gy[t][:, c * HALF : (c + 1) * HALF], y_ps[(c, t)][:], ACT.Copy, scale=gain[:, t : t + 1]
                 )
-        for c in range(2):
-            for t in range(PACK):
-                nc.scalar.activation(gy_bf[c][:, t, :], y_ps[PACK * c + t][:], ACT.Copy, scale=gain[:, t : t + 1])
+            nc.scalar.activation(gy_bf[0][:, t, :], y_ps[(0, t)][:], ACT.Copy, scale=gain[:, t : t + 1])
+        for t in range(PACK):
+            nc.scalar.activation(gy_bf[1][:, t, :], y_ps[(1, t)][:], ACT.Copy, scale=gain[:, t : t + 1])
 
         w2_dealt = keep.tile([P, PACK, P, PACK], BF16, name="w2_dealt", align_bytes=64)
         for half in range(2):
@@ -119,25 +123,22 @@ def tile_picked_laymedsendg_none_p_kernel(
         w2_scales = keep.tile([P, N], U8, name="w2_scales", align_bytes=64)
 
         h_win = [keep.tile([P, S], F32, name="h_win%d" % t) for t in range(PACK)]
+        h_own = [keep.tile([P, S], F32, name="h_own%d" % t, tag="h_own%d" % t) for t in range(FUSED)]
         gate = [keep.tile([P, S], F32, name="gate%d" % t) for t in range(PACK)]
 
         def weave(ap):
-            return ap.rearrange("p t (c i) -> p c t i", i=4)
+            return ap.rearrange("p t (c i) -> p c t i", i=RUN)
 
         def woven(ap):
-            return ap.rearrange("p (c i) t -> p c t i", i=4)
+            return ap.rearrange("p (c i) t -> p c t i", i=RUN)
 
         def fetch_y(c, t, dst, places):
-            nc.vector.tensor_copy(dst[:, t, :], gy[t][:].indirect(places[:, c * LC : (c + 1) * LC]))
+            nc.vector.tensor_copy(dst[:, t, :], gy[t][:].indirect(places[:, c * LIST_HALF : (c + 1) * LIST_HALF]))
 
-        def bounds(c, pa, pb):
-            lo = keep.tile([P, PACK, HALF], BF16, name="lo%d" % c)
-            hi = keep.tile([P, PACK, HALF], BF16, name="hi%d" % c)
-            cut = keep.tile([P, PACK, HALF], BF16, name="cut%d" % c, tag="cut0_then_pa1" if c == 0 else "cut1")
-            nc.vector.tensor_tensor(hi[:], pa[:], pb[:], ALU.max)
-            nc.vector.tensor_tensor(lo[:], pa[:], pb[:], ALU.min)
-            nc.vector.tensor_tensor(cut[:], hi[:], gy_bf[c][:], ALU.min)
-            return lo, cut
+        def pick(name, a, b, op, tag):
+            picked = keep.tile([P, PACK, HALF], BF16, name=name, tag=tag)
+            nc.vector.tensor_tensor(picked[:], a[:], b[:], op)
+            return picked
 
         def second_product(name, z, width, first_bank):
             z_codes = keep.tile([P, width], U32, name="z_codes" + name, align_bytes=64)
@@ -148,57 +149,62 @@ def tile_picked_laymedsendg_none_p_kernel(
             banks = []
             for t in range(PACK):
                 acc = psum.tile([P, width], F32, name="h_ps%s_%d" % (name, t), tag="bank%d" % (t + first_bank))
-                nc.tensor.matmul_mx(
-                    out=acc[:],
-                    lhsT=w2_codes[:, t * P : (t + 1) * P].bitcast(FP8X4),
-                    lhsT_scale=w2_scales[:, t * P : (t + 1) * P],
-                    rhs=z_codes[:].bitcast(FP8X4),
-                    rhs_scale=z_scales[:],
-                    start=True,
-                    stop=True,
-                )
+                product(acc, w2_codes, w2_scales, t, z_codes[:], z_scales[:])
                 banks.append(acc)
             return banks
 
         def leave_bank(cols, t, acc):
             nc.scalar.copy(h_win[t][:, cols], acc[:])
+            if t < FUSED:
+                nc.scalar.copy(h_own[t][:, cols], acc[:])
 
-        pa = keep.tile([P, PACK, HALF], BF16, name="pa0")
+        pa = keep.tile([P, PACK, HALF], BF16, name="pa0", tag="pa")
         pb = keep.tile([P, PACK, HALF], BF16, name="pb0")
         for t in range(PACK):
             fetch_y(0, t, pa, n1_sb)
             fetch_y(0, t, pb, n2_sb)
-        lo, cut = bounds(0, pa, pb)
-        z_planes = keep.tile([P, PACK, HALF], BF16, name="z_planes")
-        nc.vector.tensor_tensor(z_planes[:], lo[:], cut[:], ALU.max)
+        hi = pick("hi0", pa, gy_bf[0], ALU.max, "hi0")
+        lo = pick("lo0", pa, gy_bf[0], ALU.min, "lo0")
+        cut = pick("cut0", hi, pb, ALU.min, "cut0")
+        z_tiles = pick("z_tiles", lo, cut, ALU.max, "z_tiles")
         z0 = keep.tile([P, HALF, PACK], BF16, name="z0", tag="z0_then_pb1", align_bytes=64)
-        nc.scalar.copy(woven(z0[:]), weave(z_planes[:]))
+        nc.scalar.copy(woven(z0[:]), weave(z_tiles[:]))
         nc.vector.quantize_mx(
             out=w2_codes[:].bitcast(FP8X4), scales=w2_scales[:], in_=w2_dealt[:].rearrange("p t m j -> p (t m j)")
         )
-        pa = keep.tile([P, PACK, HALF], BF16, name="pa1", tag="cut0_then_pa1")
+
+        pa = keep.tile([P, PACK, HALF], BF16, name="pa1", tag="pa")
         for t in range(PACK):
             fetch_y(1, t, pa, n1_sb)
-        banks = second_product("0", z0, HALF, 0)
+        hi = pick("hi1", pa, gy_bf[1], ALU.max, "hi1")
+        early_banks = second_product("0", z0, HALF, 0)
         pb = keep.tile([P, PACK, HALF], BF16, name="pb1", tag="z0_then_pb1", align_bytes=64)
         for t in range(PACK):
             fetch_y(1, t, pb, n2_sb)
         for t in range(PACK):
-            leave_bank(slice(0, HALF), t, banks[t])
+            leave_bank(slice(0, HALF), t, early_banks[t])
         for t in range(PACK):
-            nc.scalar.activation(gate[t][:, 0:HALF], banks[t][:], ACT.Sigmoid)
-        lo, cut = bounds(1, pa, pb)
-        zq = []
+            nc.scalar.activation(gate[t][:, 0:HALF], early_banks[t][:], ACT.Sigmoid)
+
+        def cut_quarter(u):
+            cols = slice(u * QUARTER, (u + 1) * QUARTER)
+            cut_part = keep.tile([P, PACK, QUARTER], BF16, name="cut1_%d" % u)
+            nc.vector.tensor_tensor(cut_part[:], hi[:, :, cols], pb[:, :, cols], ALU.min)
+            return cut_part
+
+        cuts = [cut_quarter(0)]
+        lo = pick("lo1", pa, gy_bf[1], ALU.min, "gy2")
+        cuts.append(cut_quarter(1))
+        z1 = []
         for u in range(2):
             cols = slice(u * QUARTER, (u + 1) * QUARTER)
             z = keep.tile([P, QUARTER, PACK], BF16, name="z1_%d" % u, align_bytes=64)
-            nc.vector.tensor_tensor(woven(z[:]), weave(lo[:, :, cols]), weave(cut[:, :, cols]), ALU.max)
-            zq.append(z)
-        late_banks = [second_product("1_%d" % u, zq[u], QUARTER, PACK * (1 - u)) for u in range(2)]
+            nc.vector.tensor_tensor(woven(z[:]), weave(lo[:, :, cols]), weave(cuts[u][:]), ALU.max)
+            z1.append(z)
+        late_banks = [second_product("1_%d" % u, z1[u], QUARTER, PACK * (1 - u)) for u in range(2)]
 
         out_rows = out.rearrange("(p t) c -> p t c", t=PACK)
-        other = [keep.tile([P, S], F32, name="other%d" % t) for t in range(PACK)]
-        larger = [keep.tile([P, S], F32, name="larger%d" % t) for t in range(PACK)]
+        fetched = [keep.tile([P, S], F32, name="fetched%d" % t, tag="fetched%d" % t) for t in range(PACK)]
         sent = [keep.tile([P, 2 * S], F32, name="sent%d" % t) for t in range(PACK)]
 
         for t in range(PACK):
@@ -206,17 +212,37 @@ def tile_picked_laymedsendg_none_p_kernel(
                 leave_bank(slice(HALF + u * QUARTER, HALF + (u + 1) * QUARTER), t, late_banks[u][t])
             for c in range(2):
                 cols = slice(c * HALF, (c + 1) * HALF)
-                nc.vector.tensor_copy(other[t][:, cols], h_win[t][:].indirect(n4_sb[:, c * LC : (c + 1) * LC]))
-        for t in range(PACK):
-            rise = keep.tile([P, S], F32, name="rise%d" % t, tag="rise")
-            nc.gpsimd.tensor_tensor(rise[:], other[t][:], h_win[t][:], ALU.subtract)
+                looked_up = h_win[t][:].indirect(n4_sb[:, c * LIST_HALF : (c + 1) * LIST_HALF])
+                if t < FUSED:
+                    nc.vector.tensor_tensor(fetched[t][:, cols], looked_up, h_own[t][:, cols], ALU.subtract)
+                else:
+                    nc.vector.tensor_copy(fetched[t][:, cols], looked_up)
+
+        def excess(t, rise):
             lift = keep.tile([P, S], F32, name="lift%d" % t, tag="lift%d" % t)
             nc.scalar.activation(lift[:], rise[:], ACT.Relu)
-            nc.gpsimd.tensor_tensor(larger[t][:], lift[:], h_win[t][:], ALU.add)
-            nc.vector.tensor_copy(sent[t][:].indirect(n3_sb[:]), larger[t][:])
+            return lift
+
+        def send(t, lift, tag):
+            larger = keep.tile([P, S], F32, name="larger%d" % t, tag=tag)
+            nc.gpsimd.tensor_tensor(larger[:], lift[:], h_win[t][:], ALU.add)
+            nc.vector.tensor_copy(sent[t][:].indirect(n3_sb[:]), larger[:])
             nc.scalar.activation(gate[t][:, HALF:S], h_win[t][:, HALF:S], ACT.Sigmoid)
+
+        def rise_of(t, tag):
+            rise = keep.tile([P, S], F32, name="rise%d" % t, tag=tag)
+            nc.gpsimd.tensor_tensor(rise[:], fetched[t][:], h_win[t][:], ALU.subtract)
+            return rise
+
+        send(0, excess(0, fetched[0]), "h_own1")
+        send(1, excess(1, fetched[1]), "h_own0")
+        lift2 = excess(2, rise_of(2, "lift1"))
+        lift3 = excess(3, rise_of(3, "fetched2"))
+        send(2, lift2, "larger2")
+        send(3, lift3, "larger3")
+
         for t in range(PACK - 1):
-            res = keep.tile([P, S], F32, name="res%d" % t, tag="lift%d" % (t + 1))
+            res = keep.tile([P, S], F32, name="res%d" % t, tag="lift%d" % ((t + 2) % PACK))
             nc.gpsimd.tensor_tensor(res[:], sent[t][:, 0:S], gate[t][:], ALU.mult)
             nc.sync.dma_start(out_rows[:, t, :], res[:])
         last = PACK - 1

@@ -113,8 +113,6 @@ def tile_picked_laymedsendg_none_p_kernel(
                     gy[t][:, c * HALF : (c + 1) * HALF], y_ps[(c, t)][:], ACT.Copy, scale=gain[:, t : t + 1]
                 )
             nc.scalar.activation(gy_bf[0][:, t, :], y_ps[(0, t)][:], ACT.Copy, scale=gain[:, t : t + 1])
-        for t in range(PACK):
-            nc.scalar.activation(gy_bf[1][:, t, :], y_ps[(1, t)][:], ACT.Copy, scale=gain[:, t : t + 1])
 
         w2_dealt = keep.tile([P, PACK, P, PACK], BF16, name="w2_dealt", align_bytes=64)
         for half in range(2):
@@ -122,7 +120,7 @@ def tile_picked_laymedsendg_none_p_kernel(
         w2_codes = keep.tile([P, N], U32, name="w2_codes", align_bytes=64)
         w2_scales = keep.tile([P, N], U8, name="w2_scales", align_bytes=64)
 
-        h_win = [keep.tile([P, S], F32, name="h_win%d" % t) for t in range(PACK)]
+        h_win = [keep.tile([P, 2 * S], F32, name="h_win%d" % t) for t in range(PACK)]
         h_own = [keep.tile([P, S], F32, name="h_own%d" % t, tag="h_own%d" % t) for t in range(FUSED)]
         gate = [keep.tile([P, S], F32, name="gate%d" % t) for t in range(PACK)]
 
@@ -140,23 +138,18 @@ def tile_picked_laymedsendg_none_p_kernel(
             nc.vector.tensor_tensor(picked[:], a[:], b[:], op)
             return picked
 
-        def second_product(name, z, width, first_bank):
+        def quantize_z(name, z, width):
             z_codes = keep.tile([P, width], U32, name="z_codes" + name, align_bytes=64)
             z_scales = keep.tile([P, width], U8, name="z_scales" + name, align_bytes=64)
             nc.vector.quantize_mx(
                 out=z_codes[:].bitcast(FP8X4), scales=z_scales[:], in_=z[:].rearrange("p j t -> p (j t)")
             )
-            banks = []
-            for t in range(PACK):
-                acc = psum.tile([P, width], F32, name="h_ps%s_%d" % (name, t), tag="bank%d" % (t + first_bank))
-                product(acc, w2_codes, w2_scales, t, z_codes[:], z_scales[:])
-                banks.append(acc)
-            return banks
+            return z_codes, z_scales
 
-        def leave_bank(cols, t, acc):
-            nc.scalar.copy(h_win[t][:, cols], acc[:])
-            if t < FUSED:
-                nc.scalar.copy(h_own[t][:, cols], acc[:])
+        def second_product(name, z_mx, width, t, bank):
+            acc = psum.tile([P, width], F32, name="h_ps%s_%d" % (name, t), tag="bank%d" % bank)
+            product(acc, w2_codes, w2_scales, t, z_mx[0][:], z_mx[1][:])
+            return acc
 
         pa = keep.tile([P, PACK, HALF], BF16, name="pa0", tag="pa")
         pb = keep.tile([P, PACK, HALF], BF16, name="pb0")
@@ -169,6 +162,8 @@ def tile_picked_laymedsendg_none_p_kernel(
         z_tiles = pick("z_tiles", lo, cut, ALU.max, "z_tiles")
         z0 = keep.tile([P, HALF, PACK], BF16, name="z0", tag="z0_then_pb1", align_bytes=64)
         nc.scalar.copy(woven(z0[:]), weave(z_tiles[:]))
+        for t in range(PACK):
+            nc.scalar.activation(gy_bf[1][:, t, :], y_ps[(1, t)][:], ACT.Copy, scale=gain[:, t : t + 1])
         nc.vector.quantize_mx(
             out=w2_codes[:].bitcast(FP8X4), scales=w2_scales[:], in_=w2_dealt[:].rearrange("p t m j -> p (t m j)")
         )
@@ -177,12 +172,15 @@ def tile_picked_laymedsendg_none_p_kernel(
         for t in range(PACK):
             fetch_y(1, t, pa, n1_sb)
         hi = pick("hi1", pa, gy_bf[1], ALU.max, "hi1")
-        early_banks = second_product("0", z0, HALF, 0)
+        z0_mx = quantize_z("0", z0, HALF)
+        early_banks = [second_product("0", z0_mx, HALF, t, t) for t in range(PACK)]
         pb = keep.tile([P, PACK, HALF], BF16, name="pb1", tag="z0_then_pb1", align_bytes=64)
         for t in range(PACK):
             fetch_y(1, t, pb, n2_sb)
         for t in range(PACK):
-            leave_bank(slice(0, HALF), t, early_banks[t])
+            nc.scalar.copy(h_win[t][:, 0:HALF], early_banks[t][:])
+            if t < FUSED:
+                nc.scalar.copy(h_own[t][:, 0:HALF], early_banks[t][:])
         for t in range(PACK):
             nc.scalar.activation(gate[t][:, 0:HALF], early_banks[t][:], ACT.Sigmoid)
 
@@ -201,22 +199,30 @@ def tile_picked_laymedsendg_none_p_kernel(
             z = keep.tile([P, QUARTER, PACK], BF16, name="z1_%d" % u, align_bytes=64)
             nc.vector.tensor_tensor(woven(z[:]), weave(lo[:, :, cols]), weave(cuts[u][:]), ALU.max)
             z1.append(z)
-        late_banks = [second_product("1_%d" % u, z1[u], QUARTER, PACK * (1 - u)) for u in range(2)]
+        z1_mx = [quantize_z("1_%d" % u, z1[u], QUARTER) for u in range(2)]
+        late_banks = [
+            [second_product("1_%d" % u, z1_mx[u], QUARTER, t, t + PACK * (1 - u)) for u in range(2)]
+            for t in range(PACK)
+        ]
 
         out_rows = out.rearrange("(p t) c -> p t c", t=PACK)
         fetched = [keep.tile([P, S], F32, name="fetched%d" % t, tag="fetched%d" % t) for t in range(PACK)]
         sent = [keep.tile([P, 2 * S], F32, name="sent%d" % t) for t in range(PACK)]
 
+        late_cols = [slice(HALF + u * QUARTER, HALF + (u + 1) * QUARTER) for u in range(2)]
         for t in range(PACK):
             for u in range(2):
-                leave_bank(slice(HALF + u * QUARTER, HALF + (u + 1) * QUARTER), t, late_banks[u][t])
-            for c in range(2):
-                cols = slice(c * HALF, (c + 1) * HALF)
-                looked_up = h_win[t][:].indirect(n4_sb[:, c * LIST_HALF : (c + 1) * LIST_HALF])
-                if t < FUSED:
+                nc.scalar.copy(h_win[t][:, late_cols[u]], late_banks[t][u][:])
+            if t < FUSED:
+                for u in range(2):
+                    nc.scalar.copy(h_own[t][:, late_cols[u]], late_banks[t][u][:])
+                pieces = 2 if t == 0 else 1
+                for c in range(pieces):
+                    cols = slice(c * S // pieces, (c + 1) * S // pieces)
+                    looked_up = h_win[t][:].indirect(n4_sb[:, cols.start // 16 : cols.stop // 16])
                     nc.vector.tensor_tensor(fetched[t][:, cols], looked_up, h_own[t][:, cols], ALU.subtract)
-                else:
-                    nc.vector.tensor_copy(fetched[t][:, cols], looked_up)
+            else:
+                nc.vector.tensor_copy(fetched[t][:], h_win[t][:].indirect(n4_sb[:]))
 
         def excess(t, rise):
             lift = keep.tile([P, S], F32, name="lift%d" % t, tag="lift%d" % t)
@@ -225,13 +231,13 @@ def tile_picked_laymedsendg_none_p_kernel(
 
         def send(t, lift, tag):
             larger = keep.tile([P, S], F32, name="larger%d" % t, tag=tag)
-            nc.gpsimd.tensor_tensor(larger[:], lift[:], h_win[t][:], ALU.add)
+            nc.gpsimd.tensor_tensor(larger[:], lift[:], h_win[t][:, 0:S], ALU.add)
             nc.vector.tensor_copy(sent[t][:].indirect(n3_sb[:]), larger[:])
             nc.scalar.activation(gate[t][:, HALF:S], h_win[t][:, HALF:S], ACT.Sigmoid)
 
         def rise_of(t, tag):
             rise = keep.tile([P, S], F32, name="rise%d" % t, tag=tag)
-            nc.gpsimd.tensor_tensor(rise[:], fetched[t][:], h_win[t][:], ALU.subtract)
+            nc.gpsimd.tensor_tensor(rise[:], fetched[t][:], h_win[t][:, 0:S], ALU.subtract)
             return rise
 
         send(0, excess(0, fetched[0]), "h_own1")

from contextlib import ExitStack

import concourse.mybir as mybir

K, T, S, H, N = 512, 2048, 512, 512, 512
FLOPS = 2 * K * H * S + 2 * H * N * S

F32 = mybir.dt.float32
BF16 = mybir.dt.bfloat16
I32 = mybir.dt.int32
U32 = mybir.dt.uint32
U16 = mybir.dt.uint16
U8 = mybir.dt.uint8
FP8X4 = mybir.dt.float8_e4m3fn_x4
ALU = mybir.AluOpType
ACT = mybir.ActivationFunctionType

P = 128
PACK = 4
QUADRANT = 32
HALF = S // 2
QUARTER = S // 4
LIST_HALF = HALF // 16
RUN = 4
VECTOR_SHARE = 44
FUSED = 2


def tile_picked_laymedsendg_none_p_kernel(
    tc, x_words, x_scales, w1, gn, w2, offs, n1, n2, n3, n4, out
):
    nc = tc.nc
    with ExitStack() as ctx:
        lists = ctx.enter_context(tc.tile_pool(name="lists", bufs=1))
        keep = ctx.enter_context(tc.tile_pool(name="keep", bufs=1))
        psum = ctx.enter_context(tc.psum_pool(name="psum", bufs=1))

        def load_list(src, name):
            tile = lists.tile([P, S // 16], U16, name=name)
            nc.sync.dma_start(tile[:], src)
            return tile

        def load_weight_half(w, half, name):
            raw = keep.tile([P, PACK, HALF], F32, name=name)
            nc.sync.dma_start(raw[:], w.rearrange("(p j) c -> p j c", j=PACK)[:, :, half * HALF : (half + 1) * HALF])
            return raw

        def deal_views(dealt, raw, half, m0, m1):
            first = half * (P // 2)
            return (
                dealt[:, :, first + m0 : first + m1, :].rearrange("p t m j -> p m j t"),
                raw[:, :, PACK * m0 : PACK * m1].rearrange("p j (m t) -> p m j t", t=PACK),
            )

        def product(acc, w_codes, w_scales, t, codes, scales):
            nc.tensor.matmul_mx(
                out=acc[:],
                lhsT=w_codes[:, t * P : (t + 1) * P].bitcast(FP8X4),
                lhsT_scale=w_scales[:, t * P : (t + 1) * P],
                rhs=codes.bitcast(FP8X4),
                rhs_scale=scales,
                start=True,
                stop=True,
            )

        x_bytes = keep.tile([P, T], U8, name="x_bytes")
        nc.vector.memset(x_bytes[:].bitcast(I32), 0)
        offs_sb = load_list(offs, "offs_sb")
        x_table = keep.tile([P, T], U32, name="x_table")
        nc.sync.dma_start(x_table[:].bitcast(I32), x_words[0].rearrange("p n r -> p (n r)").bitcast(I32))
        for q in range(P // QUADRANT):
            nc.sync.dma_start(
                x_bytes[QUADRANT * q : QUADRANT * q + 4, :].bitcast(I32),
                x_scales[0, 4 * q : 4 * q + 4, :].bitcast(I32),
            )
        w1_raw = [load_weight_half(w1, half, "w1_raw%d" % half) for half in range(2)]
        gain = keep.tile([P, PACK], F32, name="gain")
        nc.sync.dma_start(gain[:], gn.rearrange("(p t) o -> p (t o)", t=PACK))
        n1_sb = load_list(n1, "n1_sb")
        n2_sb = load_list(n2, "n2_sb")
        w2_raw = [load_weight_half(w2, half, "w2_raw%d" % half) for half in range(2)]
        n4_sb = load_list(n4, "n4_sb")
        n3_sb = load_list(n3, "n3_sb")

        xq_codes = keep.tile([P, S], U32, name="xq_codes", align_bytes=64)
        xq_scales = keep.tile([P, S], U8, name="xq_scales", align_bytes=64)
        nc.vector.tensor_copy(xq_codes[:], x_table[:].indirect(offs_sb[:]))
        nc.vector.tensor_copy(xq_scales[:], x_bytes[:].indirect(offs_sb[:]))

        w1_dealt = keep.tile([P, PACK, P, PACK], BF16, name="w1_dealt", align_bytes=64)
        nc.scalar.copy(*deal_views(w1_dealt, w1_raw[0], 0, 0, P // 2))
        nc.vector.tensor_copy(*deal_views(w1_dealt, w1_raw[1], 1, 0, VECTOR_SHARE))
        nc.scalar.copy(*deal_views(w1_dealt, w1_raw[1], 1, VECTOR_SHARE, P // 2))
        w1_codes = keep.tile([P, H], U32, name="w1_codes", align_bytes=64)
        w1_scales = keep.tile([P, H], U8, name="w1_scales", align_bytes=64)
        gy = [keep.tile([P, S], F32, name="gy%d" % t, tag="gy%d" % t) for t in range(PACK)]
        gy_bf = [keep.tile([P, PACK, HALF], BF16, name="gy_bf%d" % c) for c in range(2)]
        y_ps = {}
        for t in range(PACK):
            nc.vector.quantize_mx(
                out=w1_codes[:, t * P : (t + 1) * P].bitcast(FP8X4),
                scales=w1_scales[:, t * P : (t + 1) * P],
                in_=w1_dealt[:, t, :, :].rearrange("p m j -> p (m j)"),
            )
            for c in range(2):
                cols = slice(c * HALF, (c + 1) * HALF)
                acc = psum.tile([P, HALF], F32, name="y_ps%d_%d" % (c, t), tag="bank%d" % (t + PACK * c))
                product(acc, w1_codes, w1_scales, t, xq_codes[:, cols], xq_scales[:, cols])
                y_ps[(c, t)] = acc
        for t in range(PACK):
            for c in range(2):
                nc.scalar.activation(
                    gy[t][:, c * HALF : (c + 1) * HALF], y_ps[(c, t)][:], ACT.Copy, scale=gain[:, t : t + 1]
                )
            nc.scalar.activation(gy_bf[0][:, t, :], y_ps[(0, t)][:], ACT.Copy, scale=gain[:, t : t + 1])

        w2_dealt = keep.tile([P, PACK, P, PACK], BF16, name="w2_dealt", align_bytes=64)
        for half in range(2):
            nc.scalar.copy(*deal_views(w2_dealt, w2_raw[half], half, 0, P // 2))
        w2_codes = keep.tile([P, N], U32, name="w2_codes", align_bytes=64)
        w2_scales = keep.tile([P, N], U8, name="w2_scales", align_bytes=64)

        h_win = [keep.tile([P, 2 * S], F32, name="h_win%d" % t) for t in range(PACK)]
        h_own = [keep.tile([P, S], F32, name="h_own%d" % t, tag="h_own%d" % t) for t in range(FUSED)]
        gate = [keep.tile([P, S], F32, name="gate%d" % t) for t in range(PACK)]

        def weave(ap):
            return ap.rearrange("p t (c i) -> p c t i", i=RUN)

        def woven(ap):
            return ap.rearrange("p (c i) t -> p c t i", i=RUN)

        def fetch_y(c, t, dst, places):
            nc.vector.tensor_copy(dst[:, t, :], gy[t][:].indirect(places[:, c * LIST_HALF : (c + 1) * LIST_HALF]))

        def pick(name, a, b, op, tag):
            picked = keep.tile([P, PACK, HALF], BF16, name=name, tag=tag)
            nc.vector.tensor_tensor(picked[:], a[:], b[:], op)
            return picked

        def quantize_z(name, z, width):
            z_codes = keep.tile([P, width], U32, name="z_codes" + name, align_bytes=64)
            z_scales = keep.tile([P, width], U8, name="z_scales" + name, align_bytes=64)
            nc.vector.quantize_mx(
                out=z_codes[:].bitcast(FP8X4), scales=z_scales[:], in_=z[:].rearrange("p j t -> p (j t)")
            )
            return z_codes, z_scales

        def second_product(name, z_mx, width, t, bank):
            acc = psum.tile([P, width], F32, name="h_ps%s_%d" % (name, t), tag="bank%d" % bank)
            product(acc, w2_codes, w2_scales, t, z_mx[0][:], z_mx[1][:])
            return acc

        pa = keep.tile([P, PACK, HALF], BF16, name="pa0", tag="pa")
        pb = keep.tile([P, PACK, HALF], BF16, name="pb0")
        for t in range(PACK):
            fetch_y(0, t, pa, n1_sb)
            fetch_y(0, t, pb, n2_sb)
        hi = pick("hi0", pa, gy_bf[0], ALU.max, "hi0")
        lo = pick("lo0", pa, gy_bf[0], ALU.min, "lo0")
        cut = pick("cut0", hi, pb, ALU.min, "cut0")
        z_tiles = pick("z_tiles", lo, cut, ALU.max, "z_tiles")
        z0 = keep.tile([P, HALF, PACK], BF16, name="z0", tag="z0_then_pb1", align_bytes=64)
        nc.scalar.copy(woven(z0[:]), weave(z_tiles[:]))
        for t in range(PACK):
            nc.scalar.activation(gy_bf[1][:, t, :], y_ps[(1, t)][:], ACT.Copy, scale=gain[:, t : t + 1])
        nc.vector.quantize_mx(
            out=w2_codes[:].bitcast(FP8X4), scales=w2_scales[:], in_=w2_dealt[:].rearrange("p t m j -> p (t m j)")
        )

        pa = keep.tile([P, PACK, HALF], BF16, name="pa1", tag="pa")
        for t in range(PACK):
            fetch_y(1, t, pa, n1_sb)
        hi = pick("hi1", pa, gy_bf[1], ALU.max, "hi1")
        z0_mx = quantize_z("0", z0, HALF)
        early_banks = [second_product("0", z0_mx, HALF, t, t) for t in range(PACK)]
        pb = keep.tile([P, PACK, HALF], BF16, name="pb1", tag="z0_then_pb1", align_bytes=64)
        for t in range(PACK):
            fetch_y(1, t, pb, n2_sb)
        for t in range(PACK):
            nc.scalar.copy(h_win[t][:, 0:HALF], early_banks[t][:])
            if t < FUSED:
                nc.scalar.copy(h_own[t][:, 0:HALF], early_banks[t][:])
        for t in range(PACK):
            nc.scalar.activation(gate[t][:, 0:HALF], early_banks[t][:], ACT.Sigmoid)

        def cut_quarter(u):
            cols = slice(u * QUARTER, (u + 1) * QUARTER)
            cut_part = keep.tile([P, PACK, QUARTER], BF16, name="cut1_%d" % u)
            nc.vector.tensor_tensor(cut_part[:], hi[:, :, cols], pb[:, :, cols], ALU.min)
            return cut_part

        cuts = [cut_quarter(0)]
        lo = pick("lo1", pa, gy_bf[1], ALU.min, "gy2")
        cuts.append(cut_quarter(1))
        z1 = []
        for u in range(2):
            cols = slice(u * QUARTER, (u + 1) * QUARTER)
            z = keep.tile([P, QUARTER, PACK], BF16, name="z1_%d" % u, align_bytes=64)
            nc.vector.tensor_tensor(woven(z[:]), weave(lo[:, :, cols]), weave(cuts[u][:]), ALU.max)
            z1.append(z)
        z1_mx = [quantize_z("1_%d" % u, z1[u], QUARTER) for u in range(2)]
        late_banks = [
            [second_product("1_%d" % u, z1_mx[u], QUARTER, t, t + PACK * (1 - u)) for u in range(2)]
            for t in range(PACK)
        ]

        out_rows = out.rearrange("(p t) c -> p t c", t=PACK)
        fetched = [keep.tile([P, S], F32, name="fetched%d" % t, tag="fetched%d" % t) for t in range(PACK)]
        sent = [keep.tile([P, 2 * S], F32, name="sent%d" % t) for t in range(PACK)]

        late_cols = [slice(HALF + u * QUARTER, HALF + (u + 1) * QUARTER) for u in range(2)]
        for t in range(PACK):
            for u in range(2):
                nc.scalar.copy(h_win[t][:, late_cols[u]], late_banks[t][u][:])
            if t < FUSED:
                for u in range(2):
                    nc.scalar.copy(h_own[t][:, late_cols[u]], late_banks[t][u][:])
                pieces = 2 if t == 0 else 1
                for c in range(pieces):
                    cols = slice(c * S // pieces, (c + 1) * S // pieces)
                    looked_up = h_win[t][:].indirect(n4_sb[:, cols.start // 16 : cols.stop // 16])
                    nc.vector.tensor_tensor(fetched[t][:, cols], looked_up, h_own[t][:, cols], ALU.subtract)
            else:
                nc.vector.tensor_copy(fetched[t][:], h_win[t][:].indirect(n4_sb[:]))

        def excess(t, rise):
            lift = keep.tile([P, S], F32, name="lift%d" % t, tag="lift%d" % t)
            nc.scalar.activation(lift[:], rise[:], ACT.Relu)
            return lift

        def send(t, lift, tag):
            larger = keep.tile([P, S], F32, name="larger%d" % t, tag=tag)
            nc.gpsimd.tensor_tensor(larger[:], lift[:], h_win[t][:, 0:S], ALU.add)
            nc.vector.tensor_copy(sent[t][:].indirect(n3_sb[:]), larger[:])
            nc.scalar.activation(gate[t][:, HALF:S], h_win[t][:, HALF:S], ACT.Sigmoid)

        def rise_of(t, tag):
            rise = keep.tile([P, S], F32, name="rise%d" % t, tag=tag)
            nc.gpsimd.tensor_tensor(rise[:], fetched[t][:], h_win[t][:, 0:S], ALU.subtract)
            return rise

        send(0, excess(0, fetched[0]), "h_own1")
        send(1, excess(1, fetched[1]), "h_own0")
        lift2 = excess(2, rise_of(2, "lift1"))
        lift3 = excess(3, rise_of(3, "fetched2"))
        send(2, lift2, "larger2")
        send(3, lift3, "larger3")

        for t in range(PACK - 1):
            res = keep.tile([P, S], F32, name="res%d" % t, tag="lift%d" % ((t + 2) % PACK))
            nc.gpsimd.tensor_tensor(res[:], sent[t][:, 0:S], gate[t][:], ALU.mult)
            nc.sync.dma_start(out_rows[:, t, :], res[:])
        last = PACK - 1
        for c in range(2):
            cols = slice(c * HALF, (c + 1) * HALF)
            res = keep.tile([P, HALF], F32, name="res_last%d" % c)
            nc.vector.tensor_tensor(res[:], sent[last][:, cols], gate[last][:, cols], ALU.mult)
            nc.sync.dma_start(out_rows[:, last, cols], res[:])
